import numpy as np
import ml_dtypes

BF16 = ml_dtypes.bfloat16


def bf(x):
    return np.asarray(x, np.float32).astype(BF16)


def f32(x):
    return np.asarray(x, np.float32)


def f64(x):
    return np.asarray(x).astype(np.float64)


def striped(idx):
    return np.tile(idx.reshape(-1, 16).T, (8, 1))


S, K, M, N, D, V = 1024, 512, 128, 1536, 2, 768


def setup_inputs():
    return {"table": bf(np.random.standard_normal((K, S))), "w": bf(np.random.standard_normal((K, M)) / np.sqrt(D * K)), "c": f32(0.2 + 0.8 * np.random.random_sample((1, V))), "offs": striped(np.random.permutation(np.tile(np.arange(S), 2))[:N])}


def reference(table, w, c, offs):
    idx = offs[:16].T.reshape(-1)
    x = f64(table)[:, idx]
    y = f64(w).T @ sum(x[:, t * V : (t + 1) * V] for t in range(D))
    return y * f64(c)

@@ -1,0 +1,47 @@
+import concourse.mybir as mybir
+
+BF16, F32, U16 = mybir.dt.bfloat16, mybir.dt.float32, mybir.dt.uint16
+MULT = mybir.AluOpType.mult
+
+P = 128
+S, K, M = 1024, 512, 128
+PIECES, V = 2, 768
+BLOCKS = K // P
+FLOPS = K * V * (PIECES - 1) + 2 * K * M * V + M * V
+HALF = V // 2
+
+
+def tile_gather_matmul_kernel(tc, table, w, c, offs, out):
+    nc = tc.nc
+    with (
+        tc.tile_pool(name="held", bufs=1) as held,
+        tc.psum_pool(name="psum", bufs=1) as psum,
+    ):
+        offsets = held.tile([P, PIECES * V // 16], U16, name="offsets")
+        weights = held.tile([P, BLOCKS, M], BF16, name="weights")
+        blocks = [held.tile([P, S], BF16, name=f"block{k}") for k in range(BLOCKS)]
+        factor = held.tile([P, V], F32, name="factor")
+
+        nc.sync.dma_start(offsets[:], offs)
+        nc.scalar.dma_start(weights[:], w.rearrange("(k p) m -> p k m", p=P))
+        for k in range(BLOCKS):
+            queue = nc.scalar if k % 2 else nc.sync
+            queue.dma_start(blocks[k][:], table[k * P : (k + 1) * P, :])
+        nc.scalar.dma_start(factor[:], c[0, :].partition_broadcast(P))
+
+        for start in range(0, V, HALF):
+            bank = psum.tile([P, HALF], F32, name=f"bank{start}")
+            for k in range(BLOCKS):
+                for t in range(PIECES):
+                    first = (t * V + start) // 16
+                    picked = blocks[k][:].indirect(offsets[:, first : first + HALF // 16])
+                    nc.tensor.matmul(
+                        bank[:],
+                        weights[:, k, :],
+                        picked,
+                        start=(k == 0 and t == 0),
+                        stop=(k == BLOCKS - 1 and t == PIECES - 1),
+                    )
+            result = held.tile([P, HALF], F32, name=f"result{start}")
+            nc.vector.tensor_tensor(result[:], bank[:], factor[:, start : start + HALF], MULT)
+            nc.sync.dma_start(out[:, start : start + HALF], result[:])

@@ -8,7 +8,7 @@ S, K, M = 1024, 512, 128
 PIECES, V = 2, 768
 BLOCKS = K // P
 FLOPS = K * V * (PIECES - 1) + 2 * K * M * V + M * V
-HALF = V // 2
+WIDE = 512
 
 
 def tile_gather_matmul_kernel(tc, table, w, c, offs, out):
@@ -22,19 +22,21 @@ def tile_gather_matmul_kernel(tc, table, w, c, offs, out):
         blocks = [held.tile([P, S], BF16, name=f"block{k}") for k in range(BLOCKS)]
         factor = held.tile([P, V], F32, name="factor")
 
+        features = table.rearrange("(p k) s -> p k s", k=BLOCKS)
         nc.sync.dma_start(offsets[:], offs)
-        nc.scalar.dma_start(weights[:], w.rearrange("(k p) m -> p k m", p=P))
+        nc.scalar.dma_start(weights[:], w.rearrange("(p k) m -> p k m", k=BLOCKS))
         for k in range(BLOCKS):
             queue = nc.scalar if k % 2 else nc.sync
-            queue.dma_start(blocks[k][:], table[k * P : (k + 1) * P, :])
+            queue.dma_start(blocks[k][:], features[:, k, :])
         nc.scalar.dma_start(factor[:], c[0, :].partition_broadcast(P))
 
-        for start in range(0, V, HALF):
-            bank = psum.tile([P, HALF], F32, name=f"bank{start}")
+        for start in range(0, V, WIDE):
+            columns = min(WIDE, V - start)
+            bank = psum.tile([P, columns], F32, name=f"bank{start}")
             for k in range(BLOCKS):
                 for t in range(PIECES):
                     first = (t * V + start) // 16
-                    picked = blocks[k][:].indirect(offsets[:, first : first + HALF // 16])
+                    picked = blocks[k][:].indirect(offsets[:, first : first + columns // 16])
                     nc.tensor.matmul(
                         bank[:],
                         weights[:, k, :],
@@ -42,6 +44,6 @@ def tile_gather_matmul_kernel(tc, table, w, c, offs, out):
                         start=(k == 0 and t == 0),
                         stop=(k == BLOCKS - 1 and t == PIECES - 1),
                     )
-            result = held.tile([P, HALF], F32, name=f"result{start}")
-            nc.vector.tensor_tensor(result[:], bank[:], factor[:, start : start + HALF], MULT)
-            nc.sync.dma_start(out[:, start : start + HALF], result[:])
+            result = held.tile([P, columns], F32, name=f"result{start}")
+            nc.vector.tensor_tensor(result[:], bank[:], factor[:, start : start + columns], MULT)
+            nc.sync.dma_start(out[:, start : start + columns], result[:])

@@ -24,11 +24,10 @@ def tile_gather_matmul_kernel(tc, table, w, c, offs, out):
 
         features = table.rearrange("(p k) s -> p k s", k=BLOCKS)
         nc.sync.dma_start(offsets[:], offs)
-        nc.scalar.dma_start(weights[:], w.rearrange("(p k) m -> p k m", k=BLOCKS))
+        nc.sync.dma_start(weights[:], w.rearrange("(p k) m -> p k m", k=BLOCKS))
         for k in range(BLOCKS):
-            queue = nc.scalar if k % 2 else nc.sync
-            queue.dma_start(blocks[k][:], features[:, k, :])
-        nc.scalar.dma_start(factor[:], c[0, :].partition_broadcast(P))
+            nc.sync.dma_start(blocks[k][:], features[:, k, :])
+        nc.sync.dma_start(factor[:], c[0, :].partition_broadcast(P))
 
         for start in range(0, V, WIDE):
             columns = min(WIDE, V - start)

@@ -18,15 +18,15 @@ def tile_gather_matmul_kernel(tc, table, w, c, offs, out):
         tc.psum_pool(name="psum", bufs=1) as psum,
     ):
         offsets = held.tile([P, PIECES * V // 16], U16, name="offsets")
-        weights = held.tile([P, BLOCKS, M], BF16, name="weights")
+        weights = [held.tile([P, M], BF16, name=f"weights{k}") for k in range(BLOCKS)]
         blocks = [held.tile([P, S], BF16, name=f"block{k}") for k in range(BLOCKS)]
         factor = held.tile([P, V], F32, name="factor")
 
-        features = table.rearrange("(p k) s -> p k s", k=BLOCKS)
         nc.sync.dma_start(offsets[:], offs)
-        nc.sync.dma_start(weights[:], w.rearrange("(p k) m -> p k m", k=BLOCKS))
         for k in range(BLOCKS):
-            nc.sync.dma_start(blocks[k][:], features[:, k, :])
+            features = slice(k * P, (k + 1) * P)
+            nc.sync.dma_start(weights[k][:], w[features, :])
+            nc.sync.dma_start(blocks[k][:], table[features, :])
         nc.sync.dma_start(factor[:], c[0, :].partition_broadcast(P))
 
         for start in range(0, V, WIDE):
@@ -38,7 +38,7 @@ def tile_gather_matmul_kernel(tc, table, w, c, offs, out):
                     picked = blocks[k][:].indirect(offsets[:, first : first + columns // 16])
                     nc.tensor.matmul(
                         bank[:],
-                        weights[:, k, :],
+                        weights[k][:],
                         picked,
                         start=(k == 0 and t == 0),
                         stop=(k == BLOCKS - 1 and t == PIECES - 1),

import concourse.mybir as mybir

BF16, F32, U16 = mybir.dt.bfloat16, mybir.dt.float32, mybir.dt.uint16
MULT = mybir.AluOpType.mult

P = 128
S, K, M = 1024, 512, 128
PIECES, V = 2, 768
BLOCKS = K // P
FLOPS = K * V * (PIECES - 1) + 2 * K * M * V + M * V
WIDE = 512


def tile_gather_matmul_kernel(tc, table, w, c, offs, out):
    nc = tc.nc
    with (
        tc.tile_pool(name="held", bufs=1) as held,
        tc.psum_pool(name="psum", bufs=1) as psum,
    ):
        offsets = held.tile([P, PIECES * V // 16], U16, name="offsets")
        weights = [held.tile([P, M], BF16, name=f"weights{k}") for k in range(BLOCKS)]
        blocks = [held.tile([P, S], BF16, name=f"block{k}") for k in range(BLOCKS)]
        factor = held.tile([P, V], F32, name="factor")

        nc.sync.dma_start(offsets[:], offs)
        for k in range(BLOCKS):
            features = slice(k * P, (k + 1) * P)
            nc.sync.dma_start(weights[k][:], w[features, :])
            nc.sync.dma_start(blocks[k][:], table[features, :])
        nc.sync.dma_start(factor[:], c[0, :].partition_broadcast(P))

        for start in range(0, V, WIDE):
            columns = min(WIDE, V - start)
            bank = psum.tile([P, columns], F32, name=f"bank{start}")
            for k in range(BLOCKS):
                for t in range(PIECES):
                    first = (t * V + start) // 16
                    picked = blocks[k][:].indirect(offsets[:, first : first + columns // 16])
                    nc.tensor.matmul(
                        bank[:],
                        weights[k][:],
                        picked,
                        start=(k == 0 and t == 0),
                        stop=(k == BLOCKS - 1 and t == PIECES - 1),
                    )
            result = held.tile([P, columns], F32, name=f"result{start}")
            nc.vector.tensor_tensor(result[:], bank[:], factor[:, start : start + columns], MULT)
            nc.sync.dma_start(out[:, start : start + columns], result[:])
